import numpy as np
import ml_dtypes

BF16 = ml_dtypes.bfloat16


def bf(x):
    return np.asarray(x, np.float32).astype(BF16)


def f32(x):
    return np.asarray(x, np.float32)


def f64(x):
    return np.asarray(x).astype(np.float64)


def striped(idx):
    return np.tile(idx.reshape(-1, 16).T, (8, 1))


S, K, M, N, E, Q, H = 256, 128, 512, 256, 2, 128, 256


def sigmoid(v):
    return 1.0 / (1.0 + np.exp(-v))


def setup_inputs():
    return {"table": bf(np.random.standard_normal((K, S))), "w": bf(np.random.standard_normal((E, K, M)) / np.sqrt(K)), "offs": striped(np.sort(np.random.permutation(S).reshape(E, Q), axis=1).reshape(-1))}


def reference(table, w, offs):
    idx = offs[:16].T.reshape(-1)
    x = f64(table)[:, idx]
    y = np.concatenate([f64(w)[e].T @ x[:, e * Q : (e + 1) * Q] for e in range(E)], axis=1)
    return y[:H] * sigmoid(y[H:])

@@ -1,0 +1,53 @@
+import concourse.mybir as mybir
+
+BF16, F32, U16 = mybir.dt.bfloat16, mybir.dt.float32, mybir.dt.uint16
+SIGMOID = mybir.ActivationFunctionType.Sigmoid
+MULT = mybir.AluOpType.mult
+
+P = 128
+TOKENS = 256
+EXPERTS = 2
+PIECE = 128
+HALF = 256
+BLOCKS = HALF // P
+PIECE_COLUMNS = PIECE // 16
+
+FLOPS = 2 * P * (2 * HALF) * (EXPERTS * PIECE)
+
+
+def tile_gather_matmul_kernel(tc, table, w, offs, out):
+    nc = tc.nc
+    out_blocks = out.rearrange("(a p) j -> p a j", p=P)
+
+    with (
+        tc.tile_pool(name="held", bufs=1) as held,
+        tc.psum_pool(name="psum", bufs=1) as psum,
+    ):
+        offsets = held.tile([P, EXPERTS * PIECE_COLUMNS], U16, name="offsets")
+        nc.sync.dma_start(offsets[:], offs)
+        tokens = held.tile([P, TOKENS], BF16, name="tokens")
+        nc.scalar.dma_start(tokens[:], table)
+        weights = [held.tile([P, 2 * HALF], BF16, name=f"weights{e}") for e in range(EXPERTS)]
+        nc.sync.dma_start(weights[0][:], w[0])
+        nc.scalar.dma_start(weights[1][:], w[1])
+
+        picked = [
+            tokens[:].indirect(offsets[:, e * PIECE_COLUMNS : (e + 1) * PIECE_COLUMNS])
+            for e in range(EXPERTS)
+        ]
+
+        opened = [held.tile([P, BLOCKS, PIECE], F32, name=f"opened{e}") for e in range(EXPERTS)]
+        for e in range(EXPERTS):
+            gates = psum.tile([P, BLOCKS, PIECE], F32, name=f"gates{e}")
+            for a in range(BLOCKS):
+                columns = slice(HALF + a * P, HALF + (a + 1) * P)
+                nc.tensor.matmul(gates[:, a, :], weights[e][:, columns], picked[e], start=True, stop=True)
+            nc.scalar.activation(opened[e][:], gates[:], SIGMOID)
+
+        for e in range(EXPERTS):
+            result = held.tile([P, BLOCKS, PIECE], F32, name=f"result{e}")
+            for a in range(BLOCKS):
+                values = psum.tile([P, PIECE], F32, name=f"values{e}{a}")
+                nc.tensor.matmul(values[:], weights[e][:, a * P : (a + 1) * P], picked[e], start=True, stop=True)
+                nc.vector.tensor_tensor(result[:, a, :], values[:], opened[e][:, a, :], MULT)
+            nc.sync.dma_start(out_blocks[:, :, e * PIECE : (e + 1) * PIECE], result[:])

@@ -17,7 +17,6 @@ FLOPS = 2 * P * (2 * HALF) * (EXPERTS * PIECE)
 
 def tile_gather_matmul_kernel(tc, table, w, offs, out):
     nc = tc.nc
-    out_blocks = out.rearrange("(a p) j -> p a j", p=P)
 
     with (
         tc.tile_pool(name="held", bufs=1) as held,
@@ -45,9 +44,9 @@ def tile_gather_matmul_kernel(tc, table, w, offs, out):
             nc.scalar.activation(opened[e][:], gates[:], SIGMOID)
 
         for e in range(EXPERTS):
-            result = held.tile([P, BLOCKS, PIECE], F32, name=f"result{e}")
             for a in range(BLOCKS):
                 values = psum.tile([P, PIECE], F32, name=f"values{e}{a}")
                 nc.tensor.matmul(values[:], weights[e][:, a * P : (a + 1) * P], picked[e], start=True, stop=True)
-                nc.vector.tensor_tensor(result[:, a, :], values[:], opened[e][:, a, :], MULT)
-            nc.sync.dma_start(out_blocks[:, :, e * PIECE : (e + 1) * PIECE], result[:])
+                result = held.tile([P, PIECE], F32, name=f"result{e}{a}")
+                nc.vector.tensor_tensor(result[:], values[:], opened[e][:, a, :], MULT)
+                nc.sync.dma_start(out[a * P : (a + 1) * P, e * PIECE : (e + 1) * PIECE], result[:])

@@ -11,6 +11,8 @@ PIECE = 128
 HALF = 256
 BLOCKS = HALF // P
 PIECE_COLUMNS = PIECE // 16
+WARMING = 6
+WARMING_COLUMNS = 256
 
 FLOPS = 2 * P * (2 * HALF) * (EXPERTS * PIECE)
 
@@ -29,6 +31,12 @@ def tile_gather_matmul_kernel(tc, table, w, offs, out):
         weights = [held.tile([P, 2 * HALF], BF16, name=f"weights{e}") for e in range(EXPERTS)]
         nc.sync.dma_start(weights[0][:], w[0])
         nc.scalar.dma_start(weights[1][:], w[1])
+
+        zeros = held.tile([P, WARMING_COLUMNS], BF16, name="zeros")
+        nc.vector.memset(zeros[:], 0.0)
+        unread = psum.tile([P, WARMING_COLUMNS], F32, name="unread")
+        for i in range(WARMING):
+            nc.tensor.matmul(unread[:], zeros[:, 0:P], zeros[:], start=True, stop=True)
 
         picked = [
             tokens[:].indirect(offsets[:, e * PIECE_COLUMNS : (e + 1) * PIECE_COLUMNS])

@@ -20,10 +20,7 @@ FLOPS = 2 * P * (2 * HALF) * (EXPERTS * PIECE)
 def tile_gather_matmul_kernel(tc, table, w, offs, out):
     nc = tc.nc
 
-    with (
-        tc.tile_pool(name="held", bufs=1) as held,
-        tc.psum_pool(name="psum", bufs=1) as psum,
-    ):
+    with tc.tile_pool(name="held", bufs=1) as held:
         offsets = held.tile([P, EXPERTS * PIECE_COLUMNS], U16, name="offsets")
         nc.sync.dma_start(offsets[:], offs)
         tokens = held.tile([P, TOKENS], BF16, name="tokens")
@@ -34,27 +31,31 @@ def tile_gather_matmul_kernel(tc, table, w, offs, out):
 
         zeros = held.tile([P, WARMING_COLUMNS], BF16, name="zeros")
         nc.vector.memset(zeros[:], 0.0)
-        unread = psum.tile([P, WARMING_COLUMNS], F32, name="unread")
-        for i in range(WARMING):
-            nc.tensor.matmul(unread[:], zeros[:, 0:P], zeros[:], start=True, stop=True)
+        with tc.psum_pool(name="idle", bufs=1) as idle:
+            unread = idle.tile([P, WARMING_COLUMNS], F32, name="unread")
+            for i in range(WARMING):
+                nc.tensor.matmul(unread[:], zeros[:, 0:P], zeros[:], start=True, stop=True)
 
         picked = [
             tokens[:].indirect(offsets[:, e * PIECE_COLUMNS : (e + 1) * PIECE_COLUMNS])
             for e in range(EXPERTS)
         ]
 
-        opened = [held.tile([P, BLOCKS, PIECE], F32, name=f"opened{e}") for e in range(EXPERTS)]
-        for e in range(EXPERTS):
-            gates = psum.tile([P, BLOCKS, PIECE], F32, name=f"gates{e}")
-            for a in range(BLOCKS):
-                columns = slice(HALF + a * P, HALF + (a + 1) * P)
-                nc.tensor.matmul(gates[:, a, :], weights[e][:, columns], picked[e], start=True, stop=True)
-            nc.scalar.activation(opened[e][:], gates[:], SIGMOID)
+        with tc.psum_pool(name="psum", bufs=1) as psum:
+            opened = [
+                [held.tile([P, PIECE], F32, name=f"opened{e}{a}") for a in range(BLOCKS)] for e in range(EXPERTS)
+            ]
+            for e in range(EXPERTS):
+                for a in range(BLOCKS):
+                    gates = psum.tile([P, PIECE], F32, name=f"gates{e}{a}")
+                    columns = slice(HALF + a * P, HALF + (a + 1) * P)
+                    nc.tensor.matmul(gates[:], weights[e][:, columns], picked[e], start=True, stop=True)
+                    nc.scalar.activation(opened[e][a][:], gates[:], SIGMOID)
 
-        for e in range(EXPERTS):
-            for a in range(BLOCKS):
-                values = psum.tile([P, PIECE], F32, name=f"values{e}{a}")
-                nc.tensor.matmul(values[:], weights[e][:, a * P : (a + 1) * P], picked[e], start=True, stop=True)
-                result = held.tile([P, PIECE], F32, name=f"result{e}{a}")
-                nc.vector.tensor_tensor(result[:], values[:], opened[e][:, a, :], MULT)
-                nc.sync.dma_start(out[a * P : (a + 1) * P, e * PIECE : (e + 1) * PIECE], result[:])
+            for e in range(EXPERTS):
+                for a in range(BLOCKS):
+                    values = psum.tile([P, PIECE], F32, name=f"values{e}{a}")
+                    nc.tensor.matmul(values[:], weights[e][:, a * P : (a + 1) * P], picked[e], start=True, stop=True)
+                    result = held.tile([P, PIECE], F32, name=f"result{e}{a}")
+                    nc.vector.tensor_tensor(result[:], values[:], opened[e][a][:], MULT)
+                    nc.sync.dma_start(out[a * P : (a + 1) * P, e * PIECE : (e + 1) * PIECE], result[:])

@@ -27,7 +27,7 @@ def tile_gather_matmul_kernel(tc, table, w, offs, out):
         nc.scalar.dma_start(tokens[:], table)
         weights = [held.tile([P, 2 * HALF], BF16, name=f"weights{e}") for e in range(EXPERTS)]
         nc.sync.dma_start(weights[0][:], w[0])
-        nc.scalar.dma_start(weights[1][:], w[1])
+        nc.sync.dma_start(weights[1][:], w[1])
 
         zeros = held.tile([P, WARMING_COLUMNS], BF16, name="zeros")
         nc.vector.memset(zeros[:], 0.0)
@@ -42,20 +42,16 @@ def tile_gather_matmul_kernel(tc, table, w, offs, out):
         ]
 
         with tc.psum_pool(name="psum", bufs=1) as psum:
-            opened = [
-                [held.tile([P, PIECE], F32, name=f"opened{e}{a}") for a in range(BLOCKS)] for e in range(EXPERTS)
-            ]
             for e in range(EXPERTS):
+                opened = [held.tile([P, PIECE], F32, name=f"opened{e}{a}") for a in range(BLOCKS)]
                 for a in range(BLOCKS):
                     gates = psum.tile([P, PIECE], F32, name=f"gates{e}{a}")
                     columns = slice(HALF + a * P, HALF + (a + 1) * P)
                     nc.tensor.matmul(gates[:], weights[e][:, columns], picked[e], start=True, stop=True)
-                    nc.scalar.activation(opened[e][a][:], gates[:], SIGMOID)
-
-            for e in range(EXPERTS):
+                    nc.scalar.activation(opened[a][:], gates[:], SIGMOID)
                 for a in range(BLOCKS):
                     values = psum.tile([P, PIECE], F32, name=f"values{e}{a}")
                     nc.tensor.matmul(values[:], weights[e][:, a * P : (a + 1) * P], picked[e], start=True, stop=True)
                     result = held.tile([P, PIECE], F32, name=f"result{e}{a}")
-                    nc.vector.tensor_tensor(result[:], values[:], opened[e][a][:], MULT)
+                    nc.vector.tensor_tensor(result[:], values[:], opened[a][:], MULT)
                     nc.sync.dma_start(out[a * P : (a + 1) * P, e * PIECE : (e + 1) * PIECE], result[:])

@@ -21,12 +21,12 @@ def tile_gather_matmul_kernel(tc, table, w, offs, out):
     nc = tc.nc
 
     with tc.tile_pool(name="held", bufs=1) as held:
-        offsets = held.tile([P, EXPERTS * PIECE_COLUMNS], U16, name="offsets")
-        nc.sync.dma_start(offsets[:], offs)
-        tokens = held.tile([P, TOKENS], BF16, name="tokens")
-        nc.scalar.dma_start(tokens[:], table)
         weights = [held.tile([P, 2 * HALF], BF16, name=f"weights{e}") for e in range(EXPERTS)]
         nc.sync.dma_start(weights[0][:], w[0])
+        tokens = held.tile([P, TOKENS], BF16, name="tokens")
+        nc.scalar.dma_start(tokens[:], table)
+        offsets = held.tile([P, EXPERTS * PIECE_COLUMNS], U16, name="offsets")
+        nc.sync.dma_start(offsets[:], offs)
         nc.sync.dma_start(weights[1][:], w[1])
 
         zeros = held.tile([P, WARMING_COLUMNS], BF16, name="zeros")

@@ -27,7 +27,7 @@ def tile_gather_matmul_kernel(tc, table, w, offs, out):
         nc.scalar.dma_start(tokens[:], table)
         offsets = held.tile([P, EXPERTS * PIECE_COLUMNS], U16, name="offsets")
         nc.sync.dma_start(offsets[:], offs)
-        nc.sync.dma_start(weights[1][:], w[1])
+        nc.scalar.dma_start(weights[1][:], w[1])
 
         zeros = held.tile([P, WARMING_COLUMNS], BF16, name="zeros")
         nc.vector.memset(zeros[:], 0.0)

@@ -13,6 +13,7 @@ BLOCKS = HALF // P
 PIECE_COLUMNS = PIECE // 16
 WARMING = 6
 WARMING_COLUMNS = 256
+WARMING_ROWS = 32
 
 FLOPS = 2 * P * (2 * HALF) * (EXPERTS * PIECE)
 
@@ -29,12 +30,14 @@ def tile_gather_matmul_kernel(tc, table, w, offs, out):
         nc.sync.dma_start(offsets[:], offs)
         nc.scalar.dma_start(weights[1][:], w[1])
 
-        zeros = held.tile([P, WARMING_COLUMNS], BF16, name="zeros")
+        zeros = held.tile([P, WARMING_ROWS], BF16, name="zeros")
         nc.vector.memset(zeros[:], 0.0)
         with tc.psum_pool(name="idle", bufs=1) as idle:
-            unread = idle.tile([P, WARMING_COLUMNS], F32, name="unread")
+            unread = idle.tile([WARMING_ROWS, WARMING_COLUMNS], F32, name="unread")
             for i in range(WARMING):
-                nc.tensor.matmul(unread[:], zeros[:, 0:P], zeros[:], start=True, stop=True)
+                nc.tensor.matmul(
+                    unread[:], zeros[:], zeros[:, 0:1].to_broadcast([P, WARMING_COLUMNS]), start=True, stop=True
+                )
 
         picked = [
             tokens[:].indirect(offsets[:, e * PIECE_COLUMNS : (e + 1) * PIECE_COLUMNS])

@@ -11,7 +11,7 @@ PIECE = 128
 HALF = 256
 BLOCKS = HALF // P
 PIECE_COLUMNS = PIECE // 16
-WARMING = 6
+WARMING = 4
 WARMING_COLUMNS = 256
 WARMING_ROWS = 32
 

@@ -11,9 +11,6 @@ PIECE = 128
 HALF = 256
 BLOCKS = HALF // P
 PIECE_COLUMNS = PIECE // 16
-WARMING = 4
-WARMING_COLUMNS = 256
-WARMING_ROWS = 32
 
 FLOPS = 2 * P * (2 * HALF) * (EXPERTS * PIECE)
 
@@ -29,15 +26,6 @@ def tile_gather_matmul_kernel(tc, table, w, offs, out):
         offsets = held.tile([P, EXPERTS * PIECE_COLUMNS], U16, name="offsets")
         nc.sync.dma_start(offsets[:], offs)
         nc.scalar.dma_start(weights[1][:], w[1])
-
-        zeros = held.tile([P, WARMING_ROWS], BF16, name="zeros")
-        nc.vector.memset(zeros[:], 0.0)
-        with tc.psum_pool(name="idle", bufs=1) as idle:
-            unread = idle.tile([WARMING_ROWS, WARMING_COLUMNS], F32, name="unread")
-            for i in range(WARMING):
-                nc.tensor.matmul(
-                    unread[:], zeros[:], zeros[:, 0:1].to_broadcast([P, WARMING_COLUMNS]), start=True, stop=True
-                )
 
         picked = [
             tokens[:].indirect(offsets[:, e * PIECE_COLUMNS : (e + 1) * PIECE_COLUMNS])

@@ -19,13 +19,18 @@ def tile_gather_matmul_kernel(tc, table, w, offs, out):
     nc = tc.nc
 
     with tc.tile_pool(name="held", bufs=1) as held:
-        weights = [held.tile([P, 2 * HALF], BF16, name=f"weights{e}") for e in range(EXPERTS)]
-        nc.sync.dma_start(weights[0][:], w[0])
+        first_gates = held.tile([P, HALF], BF16, name="first_gates")
+        nc.sync.dma_start(first_gates[:], w[0][:, HALF : 2 * HALF])
         tokens = held.tile([P, TOKENS], BF16, name="tokens")
         nc.scalar.dma_start(tokens[:], table)
         offsets = held.tile([P, EXPERTS * PIECE_COLUMNS], U16, name="offsets")
         nc.sync.dma_start(offsets[:], offs)
-        nc.scalar.dma_start(weights[1][:], w[1])
+        first_values = held.tile([P, HALF], BF16, name="first_values")
+        nc.scalar.dma_start(first_values[:], w[0][:, 0:HALF])
+        second = held.tile([P, 2 * HALF], BF16, name="second")
+        nc.sync.dma_start(second[:], w[1])
+        gate_weights = [first_gates[:], second[:, HALF : 2 * HALF]]
+        value_weights = [first_values[:], second[:, 0:HALF]]
 
         picked = [
             tokens[:].indirect(offsets[:, e * PIECE_COLUMNS : (e + 1) * PIECE_COLUMNS])
@@ -34,15 +39,19 @@ def tile_gather_matmul_kernel(tc, table, w, offs, out):
 
         with tc.psum_pool(name="psum", bufs=1) as psum:
             for e in range(EXPERTS):
+                final_expert = e == EXPERTS - 1
                 opened = [held.tile([P, PIECE], F32, name=f"opened{e}{a}") for a in range(BLOCKS)]
                 for a in range(BLOCKS):
                     gates = psum.tile([P, PIECE], F32, name=f"gates{e}{a}")
-                    columns = slice(HALF + a * P, HALF + (a + 1) * P)
-                    nc.tensor.matmul(gates[:], weights[e][:, columns], picked[e], start=True, stop=True)
+                    nc.tensor.matmul(gates[:], gate_weights[e][:, a * P : (a + 1) * P], picked[e], start=True, stop=True)
                     nc.scalar.activation(opened[a][:], gates[:], SIGMOID)
+                result = held.tile([P, BLOCKS, PIECE], F32, name=f"result{e}")
+                stored = out[:, e * PIECE : (e + 1) * PIECE].rearrange("(a p) j -> p a j", p=P)
                 for a in range(BLOCKS):
                     values = psum.tile([P, PIECE], F32, name=f"values{e}{a}")
-                    nc.tensor.matmul(values[:], weights[e][:, a * P : (a + 1) * P], picked[e], start=True, stop=True)
-                    result = held.tile([P, PIECE], F32, name=f"result{e}{a}")
-                    nc.vector.tensor_tensor(result[:], values[:], opened[a][:], MULT)
-                    nc.sync.dma_start(out[a * P : (a + 1) * P, e * PIECE : (e + 1) * PIECE], result[:])
+                    nc.tensor.matmul(values[:], value_weights[e][:, a * P : (a + 1) * P], picked[e], start=True, stop=True)
+                    nc.vector.tensor_tensor(result[:, a, :], values[:], opened[a][:], MULT)
+                    if final_expert:
+                        nc.sync.dma_start(stored[:, a, :], result[:, a, :])
+                if not final_expert:
+                    nc.sync.dma_start(stored, result[:])

import concourse.mybir as mybir

BF16, F32, U16 = mybir.dt.bfloat16, mybir.dt.float32, mybir.dt.uint16
SIGMOID = mybir.ActivationFunctionType.Sigmoid
MULT = mybir.AluOpType.mult

P = 128
TOKENS = 256
EXPERTS = 2
PIECE = 128
HALF = 256
BLOCKS = HALF // P
PIECE_COLUMNS = PIECE // 16

FLOPS = 2 * P * (2 * HALF) * (EXPERTS * PIECE)


def tile_gather_matmul_kernel(tc, table, w, offs, out):
    nc = tc.nc

    with tc.tile_pool(name="held", bufs=1) as held:
        first_gates = held.tile([P, HALF], BF16, name="first_gates")
        nc.sync.dma_start(first_gates[:], w[0][:, HALF : 2 * HALF])
        tokens = held.tile([P, TOKENS], BF16, name="tokens")
        nc.scalar.dma_start(tokens[:], table)
        offsets = held.tile([P, EXPERTS * PIECE_COLUMNS], U16, name="offsets")
        nc.sync.dma_start(offsets[:], offs)
        first_values = held.tile([P, HALF], BF16, name="first_values")
        nc.scalar.dma_start(first_values[:], w[0][:, 0:HALF])
        second = held.tile([P, 2 * HALF], BF16, name="second")
        nc.sync.dma_start(second[:], w[1])
        gate_weights = [first_gates[:], second[:, HALF : 2 * HALF]]
        value_weights = [first_values[:], second[:, 0:HALF]]

        picked = [
            tokens[:].indirect(offsets[:, e * PIECE_COLUMNS : (e + 1) * PIECE_COLUMNS])
            for e in range(EXPERTS)
        ]

        with tc.psum_pool(name="psum", bufs=1) as psum:
            for e in range(EXPERTS):
                final_expert = e == EXPERTS - 1
                opened = [held.tile([P, PIECE], F32, name=f"opened{e}{a}") for a in range(BLOCKS)]
                for a in range(BLOCKS):
                    gates = psum.tile([P, PIECE], F32, name=f"gates{e}{a}")
                    nc.tensor.matmul(gates[:], gate_weights[e][:, a * P : (a + 1) * P], picked[e], start=True, stop=True)
                    nc.scalar.activation(opened[a][:], gates[:], SIGMOID)
                result = held.tile([P, BLOCKS, PIECE], F32, name=f"result{e}")
                stored = out[:, e * PIECE : (e + 1) * PIECE].rearrange("(a p) j -> p a j", p=P)
                for a in range(BLOCKS):
                    values = psum.tile([P, PIECE], F32, name=f"values{e}{a}")
                    nc.tensor.matmul(values[:], value_weights[e][:, a * P : (a + 1) * P], picked[e], start=True, stop=True)
                    nc.vector.tensor_tensor(result[:, a, :], values[:], opened[a][:], MULT)
                    if final_expert:
                        nc.sync.dma_start(stored[:, a, :], result[:, a, :])
                if not final_expert:
                    nc.sync.dma_start(stored, result[:])
